import numpy as np
import ml_dtypes


def mxq(x, axis, fmt="e4m3"):
    dtype, down = {"e4m3": (ml_dtypes.float8_e4m3fn, 7), "e5m2": (ml_dtypes.float8_e5m2, 14)}[fmt]
    v = np.moveaxis(np.asarray(x, np.float32).astype(ml_dtypes.bfloat16).astype(np.float64), axis, -1)
    blocks = v.reshape(v.shape[:-1] + (-1, 32))
    amax = np.abs(blocks).max(-1, keepdims=True)
    byte = np.maximum(np.where(amax > 0, np.frexp(amax)[1] - 1 + 127, 0) - down, 1)
    scale = np.exp2(byte - 127.0)
    codes = (blocks / scale).astype(np.float32).astype(dtype).astype(np.float64)
    return np.moveaxis((codes * scale).reshape(v.shape), -1, axis)


WIDE = False


def mx_kscale(k):
    if not WIDE:
        return np.ones(k)
    levels = np.array([10, -10, 5, -5, 0])
    if k % 512:
        return np.exp2(np.random.permutation(np.resize(levels, k // 32))).repeat(32)
    a = np.empty((k // 512, 16))
    for p in range(k // 512):
        a[p, :8] = np.random.permutation(np.resize(levels, 8))
        for g in range(8):
            far = levels[np.abs(levels - a[p, g]) >= 10]
            a[p, g + 8] = far[np.random.randint(len(far))]
    return np.exp2(a.ravel()).repeat(32)


def f64(x):
    return np.asarray(x).astype(np.float64)


def striped(idx):
    return np.tile(idx.reshape(-1, 16).T, (8, 1)).astype(np.uint16)


def unstriped(offs):
    return offs[:16].T.reshape(-1).astype(np.int64)


E2M1 = np.array([0.0, 0.5, 1.0, 1.5, 2.0, 3.0, 4.0, 6.0, -0.0, -0.5, -1.0, -1.5, -2.0, -3.0, -4.0, -6.0])


def pack_weight(w, fmt):
    k, n = w.shape
    w = f64(np.asarray(w, np.float32).astype(ml_dtypes.bfloat16)).reshape(k // 32, 32, n)
    amax = np.abs(w).max(1)
    if fmt == "e4m3":
        byte = np.frexp(amax)[1] - 1 + 127 - 7
    else:
        mant, ex = np.frexp(amax / 6.0)
        byte = np.where(mant > 0.5, ex, ex - 1) + 127
    byte = np.clip(np.where(amax > 0, byte, 1), 1, 254)
    scaled = (w * np.exp2(127.0 - byte)[:, None, :]).reshape(k, n).astype(np.float32)
    by_word = np.ascontiguousarray(scaled.reshape(k // 512, 128, 4, n).transpose(0, 1, 3, 2))
    if fmt == "e4m3":
        words = by_word.astype(ml_dtypes.float8_e4m3fn).view(np.uint8)
    else:
        c = by_word.astype(ml_dtypes.float4_e2m1fn).view(np.uint8) & 0xF
        words = (c[..., 0::2] | (c[..., 1::2] << 4)).reshape(k // 512, 128, 2 * n)
    return np.ascontiguousarray(words), np.ascontiguousarray(byte.astype(np.uint8).reshape(k // 512, 16, n))


def unpack_weight(words, scales, fmt):
    g, _, n = scales.shape
    words = np.ascontiguousarray(words).reshape(g, 128, n, -1)
    if fmt == "e4m3":
        vals = words.view(ml_dtypes.float8_e4m3fn).astype(np.float64)
    else:
        nib = np.empty((g, 128, n, 4), np.uint8)
        nib[..., 0::2] = words & 0xF
        nib[..., 1::2] = words >> 4
        vals = E2M1[nib]
    vals = vals * np.repeat(np.exp2(scales.astype(np.float64) - 127.0), 8, axis=1)[..., None]
    return vals.transpose(0, 1, 3, 2).reshape(g * 512, n)


def gelu(v):
    return 0.5 * v * (1.0 + np.tanh(np.sqrt(2.0 / np.pi) * (v + 0.044715 * v**3)))


K, T, S, H, T3, S2, P = 1536, 2048, 1024, 512, 2048, 1024, 512

def setup_inputs():
    n = np.random.standard_normal
    s = mx_kscale(K)[:, None]
    u = mx_kscale(H)[:, None]
    tab_words, tab_scales = pack_weight(n((K, T)) * s, "e4m3")
    tab2_words, tab2_scales = pack_weight(n((H, T3)) / np.sqrt(H) / u, "e4m3")
    w1 = 0.8 * n((K, H)) / np.sqrt(K) / s * u.T
    w4_words, w4_scales = pack_weight(0.8 * n((K, H)) / np.sqrt(K) / s * u.T, "e2m1")
    return {
        "tab_words": tab_words, "tab_scales": tab_scales,
        "offs": striped(np.random.permutation(T)[:S]),
        "tab2_words": tab2_words, "tab2_scales": tab2_scales,
        "offs2": striped(np.random.permutation(T3)[:S2]),
        "pos1": striped(np.random.permutation(S)[:P]),
        "pos2": striped(np.random.permutation(S)[:P]),
        "w1": w1.astype(np.float32),
        "w4_words": w4_words, "w4_scales": w4_scales,
        "steep": np.random.uniform(1, 3, S2).astype(np.float32),
        "share": np.random.uniform(0.1, 0.5, S2).astype(np.float32),
        "base": (0.6 * n(S2)).astype(np.float32),
    }

def reference(tab_words, tab_scales, offs, tab2_words, tab2_scales, offs2, pos1, pos2,
              w1, w4_words, w4_scales, steep, share, base):
    v = unpack_weight(tab_words, tab_scales, "e4m3")[:, unstriped(offs)]
    v2 = unpack_weight(tab2_words, tab2_scales, "e4m3")[:, unstriped(offs2)]
    w4 = unpack_weight(w4_words, w4_scales, "e2m1")
    f1 = mxq(f64(w1), 0, "e4m3").T @ v
    f2 = w4.T @ v
    h = np.maximum(f1, f2)
    e = v2.T @ mxq(h, 0, "e4m3")
    top = e.max(axis=1)
    a = 1.0 / (1.0 + np.exp(-f64(steep)[:, None] * (e[:, unstriped(pos1)] - f64(share)[:, None] * top[:, None])))
    c = e[:, unstriped(pos2)] - f64(base)[:, None]
    return a * c

@@ -1,0 +1,312 @@
+from contextlib import ExitStack
+
+import concourse.mybir as mybir
+
+K, T, S, H, T3, S2, PICK = 1536, 2048, 1024, 512, 2048, 1024, 512
+FLOPS = 2 * (2 * K * H * S) + 2 * H * S2 * S
+
+F32 = mybir.dt.float32
+BF16 = mybir.dt.bfloat16
+I32 = mybir.dt.int32
+U32 = mybir.dt.uint32
+U16 = mybir.dt.uint16
+U8 = mybir.dt.uint8
+FP8X4 = mybir.dt.float8_e4m3fn_x4
+FP4X4 = mybir.dt.float4_e2m1fn_x4
+ALU = mybir.AluOpType
+ACT = mybir.ActivationFunctionType
+
+P = 128
+PACK = 4
+PASSES = K // (P * PACK)
+BANK = 512
+HALVES = S // BANK
+CHUNK = BANK // PACK
+CHUNKS = S // CHUNK
+ROW_TILES = S2 // P
+LIVE_ROWS = 100
+STREAM_BUFS = 4
+
+
+def tile_list_infrared_window_scores_kernel(
+    tc, tab_words, tab_scales, offs, tab2_words, tab2_scales, offs2, pos1, pos2,
+    w1, w4_words, w4_scales, steep, share, base, out,
+):
+    nc = tc.nc
+    with ExitStack() as ctx:
+        lists = ctx.enter_context(tc.tile_pool(name="lists", bufs=1))
+        keep = ctx.enter_context(tc.tile_pool(name="keep", bufs=1))
+        stream = ctx.enter_context(tc.tile_pool(name="stream", bufs=STREAM_BUFS))
+        ring = ctx.enter_context(tc.tile_pool(name="ring", bufs=3))
+        psum = ctx.enter_context(tc.psum_pool(name="psum", bufs=8))
+
+        def held(shape, dtype, name):
+            return keep.tile(shape, dtype, name=name, align_bytes=64)
+
+        def zero(tile):
+            nc.vector.memset(tile[:].bitcast(I32), 0)
+
+        def load_list(src, name):
+            tile = lists.tile(list(src.shape), U16, name=name)
+            nc.sync.dma_start(tile[:], src)
+            return tile
+
+        def load_scale_rows(queue, tile, scales):
+            passes = scales.shape[0]
+            for q in range(4):
+                queue.dma_start(
+                    out=tile[32 * q : 32 * q + 4 * passes, :].bitcast(I32),
+                    in_=scales[:, 4 * q : 4 * q + 4, :].bitcast(I32),
+                )
+
+        def load_words(words, name):
+            tile = stream.tile([P, T], I32, name=name, tag="stream")
+            nc.sync.dma_start(out=tile[:], in_=words.rearrange("p t i -> p (t i)").bitcast(I32))
+            return tile
+
+        def gather_words(dst, window, index, first, count):
+            nc.vector.tensor_copy(
+                out=dst[:, first % BANK : first % BANK + count],
+                in_=window[:].bitcast(U32).indirect(index[:, first // 16 : (first + count) // 16]),
+            )
+
+        def shift_rows(dst, src, a):
+            nc.sync.dma_start(
+                out=dst[0:LIVE_ROWS, :].bitcast(I32), in_=src[4 * a : 4 * a + LIVE_ROWS, :].bitcast(I32)
+            )
+
+        tab_sc_win = held([P, T], U8, "tab_sc_win")
+        nc.gpsimd.memset(tab_sc_win[:].bitcast(I32), 0)
+        w4_sc_raw = held([P, H], U8, "w4_sc_raw")
+        nc.gpsimd.memset(w4_sc_raw[:].bitcast(I32), 0)
+        tab2_sc_win = held([P, T3], U8, "tab2_sc_win")
+        zero(tab2_sc_win)
+        v_sc = [held([P, S], U8, "v_sc%d" % a) for a in range(PASSES)]
+        w4_sc = [held([P, H], U8, "w4_sc%d" % a) for a in range(PASSES)]
+        for a in range(1, PASSES):
+            zero(v_sc[a])
+            zero(w4_sc[a])
+
+        def load_w1(a):
+            raw = stream.tile([P, PACK, H], F32, name="w1_raw%d" % a, tag="stream")
+            nc.sync.dma_start(out=raw[:], in_=w1[a * 512 : (a + 1) * 512, :].rearrange("(p j) c -> p j c", j=PACK))
+            return raw
+
+        v = [[held([P, BANK], U32, "bands%d_%d" % (a, hf)) for hf in range(HALVES)] for a in range(PASSES)]
+        v2 = [held([P, BANK], U32, "samples%d" % hf) for hf in range(HALVES)]
+        w1_codes = [held([P, H], U32, "w1_codes%d" % a) for a in range(PASSES)]
+        w1_sc = [held([P, H], U8, "w1_sc%d" % a) for a in range(PASSES)]
+        w1_bf = [held([P, PACK * H], BF16, "w1_bf%d" % a) for a in range(PASSES)]
+        w4_codes = [held([P, H], U16, "w4_codes%d" % a) for a in range(PASSES)]
+
+        def round_w1(a, raw):
+            nc.scalar.copy(
+                out=w1_bf[a][:].rearrange("p (t m j) -> p m j t", t=PACK, j=PACK),
+                in_=raw[:].rearrange("p j (m t) -> p m j t", t=PACK),
+            )
+
+        def quantize_w1(a):
+            nc.vector.quantize_mx(out=w1_codes[a][:].bitcast(FP8X4), scales=w1_sc[a][:], in_=w1_bf[a][:])
+
+        def deal_w4(a):
+            nc.scalar.copy(
+                out=w4_codes[a][:].rearrange("p (t m) -> p t m", t=PACK),
+                in_=w4_raw[:, a, :].bitcast(U16).rearrange("p (m t) -> p t m", t=PACK),
+            )
+
+        def reading(bank, c, a, codes, scales, dtype, moving_scales):
+            hf, n0 = divmod(c * CHUNK, BANK)
+            for t in range(PACK):
+                cols = slice(t * P, (t + 1) * P)
+                nc.tensor.matmul_mx(
+                    out=bank[:, t * CHUNK : (t + 1) * CHUNK],
+                    lhsT=codes[:, cols].bitcast(dtype),
+                    lhsT_scale=scales[:, cols],
+                    rhs=v[a][hf][:, n0 : n0 + CHUNK].bitcast(FP8X4),
+                    rhs_scale=moving_scales[:, c * CHUNK : (c + 1) * CHUNK],
+                    start=(a == 0 and t == 0),
+                    stop=(a == PASSES - 1 and t == PACK - 1),
+                )
+
+        f1_banks = {}
+        f2_banks = {}
+
+        def f1_pass(c, a):
+            if a == 0:
+                f1_banks[c] = psum.tile([P, BANK], F32, name="bank")
+            reading(f1_banks[c], c, a, w1_codes[a], w1_sc[a], FP8X4, v_sc[0][4 * a : P, :])
+
+        def f2_pass(c, a):
+            if a == 0:
+                f2_banks[c] = psum.tile([P, BANK], F32, name="bank")
+            reading(f2_banks[c], c, a, w4_codes[a], w4_sc[a], FP4X4, v_sc[a])
+
+        def woven(bank):
+            return bank[:].rearrange("p (t n) -> p n t", t=PACK)
+
+        h_bf = [held([P, PACK * BANK], BF16, "h_bf%d" % hf) for hf in range(HALVES)]
+        h_codes = [held([P, BANK], U32, "h_codes%d" % hf) for hf in range(HALVES)]
+        h_sc = [held([P, BANK], U8, "h_sc%d" % hf) for hf in range(HALVES)]
+
+        def join(c):
+            hf, n0 = divmod(c * CHUNK, BANK)
+            f2 = ring.tile([P, BANK], F32, name="f2")
+            nc.scalar.copy(out=f2[:].rearrange("p (n t) -> p n t", t=PACK), in_=woven(f2_banks[c]))
+            nc.vector.tensor_tensor(
+                out=h_bf[hf][:, PACK * n0 : PACK * (n0 + CHUNK)].rearrange("p (n t) -> p n t", t=PACK),
+                in0=woven(f1_banks[c]),
+                in1=f2[:].rearrange("p (n t) -> p n t", t=PACK),
+                op=ALU.max,
+            )
+
+        def quantize_h(hf):
+            nc.vector.quantize_mx(out=h_codes[hf][:].bitcast(FP8X4), scales=h_sc[hf][:], in_=h_bf[hf][:])
+
+        first_chunks = range(CHUNKS // HALVES)
+
+        idx = load_list(offs, "idx")
+        load_scale_rows(nc.gpsimd, tab_sc_win, tab_scales)
+        win = load_words(tab_words[0], "tab_win0")
+        raw = load_w1(0)
+        load_scale_rows(nc.gpsimd, w4_sc_raw, w4_scales)
+        idx2 = load_list(offs2, "idx2")
+        load_scale_rows(nc.sync, tab2_sc_win, tab2_scales)
+        w4_raw = held([P, PASSES, H // 2], I32, "w4_raw")
+        nc.sync.dma_start(out=w4_raw[:], in_=w4_words.rearrange("a p c -> p a c").bitcast(I32))
+        for hf in range(HALVES):
+            gather_words(v[0][hf], win, idx, hf * BANK, BANK)
+        nc.vector.tensor_copy(out=v_sc[0][:], in_=tab_sc_win[:].indirect(idx[:]))
+        round_w1(0, raw)
+        quantize_w1(0)
+        nc.vector.tensor_copy(
+            out=w4_sc[0][:].rearrange("p (t m) -> p t m", t=PACK),
+            in_=w4_sc_raw[:].rearrange("p (m t) -> p t m", t=PACK),
+        )
+        for a in range(PASSES):
+            deal_w4(a)
+        for a in range(1, PASSES):
+            shift_rows(v_sc[a], v_sc[0], a)
+            shift_rows(w4_sc[a], w4_sc[0], a)
+        for c in first_chunks:
+            f2_pass(c, 0)
+            f1_pass(c, 0)
+
+        win = load_words(tab_words[1], "tab_win1")
+        raw = load_w1(1)
+        for hf in range(HALVES):
+            gather_words(v[1][hf], win, idx, hf * BANK, BANK)
+        round_w1(1, raw)
+        quantize_w1(1)
+        v2_sc = held([P, S2], U8, "v2_sc")
+        nc.vector.tensor_copy(out=v2_sc[:], in_=tab2_sc_win[:].indirect(idx2[:]))
+        for c in first_chunks:
+            f2_pass(c, 1)
+        for c in first_chunks:
+            f1_pass(c, 1)
+
+        raw = load_w1(2)
+        win = load_words(tab_words[2], "tab_win2")
+        tab2_win = load_words(tab2_words[0], "tab2_win")
+        p1 = load_list(pos1, "p1")
+        p2 = load_list(pos2, "p2")
+        rowwise = stream.tile([P, 3, ROW_TILES], F32, name="rowwise", tag="stream")
+        steep_c, share_c, base_c = rowwise[:, 0, :], rowwise[:, 1, :], rowwise[:, 2, :]
+        with nc.allow_non_contiguous_dma(reason="one value a row, a row a partition"):
+            for cols, vec in ((steep_c, steep), (share_c, share), (base_c, base)):
+                nc.sync.dma_start(out=cols, in_=vec.rearrange("(m p) -> p m", p=P))
+        round_w1(2, raw)
+        quantize_w1(2)
+        gather_words(v[2][0], win, idx, 0, BANK // 2)
+        gather_words(v[2][0], win, idx, BANK // 2, BANK // 2)
+        for c in first_chunks:
+            f2_pass(c, 2)
+            f1_pass(c, 2)
+            join(c)
+            if c == 0:
+                gather_words(v[2][1], win, idx, BANK, BANK)
+        gather_words(v2[0], tab2_win, idx2, 0, BANK)
+        quantize_h(0)
+        gather_words(v2[1], tab2_win, idx2, BANK, BANK)
+        slope = held([P, ROW_TILES], F32, "slope")
+        steep_share = held([P, ROW_TILES], F32, "steep_share")
+        nc.gpsimd.tensor_tensor(out=steep_share[:], in0=steep_c, in1=share_c, op=ALU.mult)
+        nc.gpsimd.tensor_scalar(
+            out=slope[:], in0=steep_share[:], scalar1=-1.0, scalar2=0.0, op0=ALU.mult, op1=ALU.add
+        )
+
+        half_top = held([P, ROW_TILES, HALVES], F32, "half_top")
+        gate_bias = held([P, ROW_TILES], F32, "gate_bias")
+        scores = {}
+        gates = {}
+        picked = {}
+
+        def score(m, hf):
+            if hf == 0:
+                scores[m] = ring.tile([P, S], F32, name="scores", bufs=ROW_TILES)
+            part, m0 = divmod(m * P, BANK)
+            bank = psum.tile([P, BANK], F32, name="bank")
+            nc.tensor.matmul_mx(
+                out=bank[:],
+                lhsT=v2[part][:, m0 : m0 + P].bitcast(FP8X4),
+                lhsT_scale=v2_sc[:, m * P : (m + 1) * P],
+                rhs=h_codes[hf][:].bitcast(FP8X4),
+                rhs_scale=h_sc[hf][:],
+                start=True,
+                stop=True,
+            )
+            nc.vector.tensor_scalar(
+                out=scores[m][:, hf * BANK : (hf + 1) * BANK], in0=bank[:], scalar1=1.0, scalar2=None,
+                op0=ALU.mult, op1=ALU.max, accum_out=half_top[:, m, hf : hf + 1],
+            )
+
+        def look(m):
+            nc.gpsimd.tensor_scalar(
+                out=gate_bias[:, m : m + 1], in0=half_top[:, m, 0:1], scalar1=half_top[:, m, 1:2],
+                scalar2=slope[:, m : m + 1], op0=ALU.max, op1=ALU.mult,
+            )
+            gates[m] = ring.tile([P, PICK], F32, name="gate")
+            nc.scalar.activation(
+                out=gates[m][:], in_=scores[m][:].indirect(p1[:]), func=ACT.Sigmoid,
+                bias=gate_bias[:, m : m + 1], scale=steep_c[:, m : m + 1],
+            )
+
+        def pick(m):
+            picked[m] = ring.tile([P, PICK], F32, name="picked")
+            nc.vector.tensor_copy(out=picked[m][:], in_=scores[m][:].indirect(p2[:]))
+
+        def finish(m):
+            result = ring.tile([P, PICK], F32, name="result")
+            nc.vector.scalar_tensor_tensor(
+                out=result[:], in0=picked[m][:], scalar=base_c[:, m : m + 1], in1=gates[m][:],
+                op0=ALU.subtract, op1=ALU.mult,
+            )
+            nc.sync.dma_start(out=out[m * P : (m + 1) * P, :], in_=result[:])
+
+        def chunk(c):
+            for a in range(PASSES):
+                f2_pass(c, a)
+            for a in range(PASSES):
+                f1_pass(c, a)
+            join(c)
+
+        chunk(4)
+        chunk(5)
+        for m in range(0, 4):
+            score(m, 0)
+        chunk(6)
+        for m in range(4, 6):
+            score(m, 0)
+        chunk(7)
+        score(6, 0)
+        quantize_h(1)
+        score(7, 0)
+        score(0, 1)
+        look(0)
+        for m in range(ROW_TILES):
+            if m + 1 < ROW_TILES:
+                score(m + 1, 1)
+                look(m + 1)
+            pick(m)
+            if m > 0:
+                finish(m - 1)
+        finish(ROW_TILES - 1)

@@ -25,7 +25,8 @@ CHUNK = BANK // PACK
 CHUNKS = S // CHUNK
 ROW_TILES = S2 // P
 LIVE_ROWS = 100
-STREAM_BUFS = 4
+STREAM_BUFS = 5
+VECTOR_FINISHES = 1
 
 
 def tile_list_infrared_window_scores_kernel(
@@ -51,10 +52,10 @@ def tile_list_infrared_window_scores_kernel(
             nc.sync.dma_start(tile[:], src)
             return tile
 
-        def load_scale_rows(queue, tile, scales):
+        def load_scale_rows(tile, scales):
             passes = scales.shape[0]
             for q in range(4):
-                queue.dma_start(
+                nc.sync.dma_start(
                     out=tile[32 * q : 32 * q + 4 * passes, :].bitcast(I32),
                     in_=scales[:, 4 * q : 4 * q + 4, :].bitcast(I32),
                 )
@@ -66,13 +67,13 @@ def tile_list_infrared_window_scores_kernel(
 
         def gather_words(dst, window, index, first, count):
             nc.vector.tensor_copy(
-                out=dst[:, first % BANK : first % BANK + count],
+                out=dst,
                 in_=window[:].bitcast(U32).indirect(index[:, first // 16 : (first + count) // 16]),
             )
 
-        def shift_rows(dst, src, a):
+        def shift_rows(dst, src, first):
             nc.sync.dma_start(
-                out=dst[0:LIVE_ROWS, :].bitcast(I32), in_=src[4 * a : 4 * a + LIVE_ROWS, :].bitcast(I32)
+                out=dst[0:LIVE_ROWS, :].bitcast(I32), in_=src[first : first + LIVE_ROWS, :].bitcast(I32)
             )
 
         tab_sc_win = held([P, T], U8, "tab_sc_win")
@@ -80,28 +81,30 @@ def tile_list_infrared_window_scores_kernel(
         w4_sc_raw = held([P, H], U8, "w4_sc_raw")
         nc.gpsimd.memset(w4_sc_raw[:].bitcast(I32), 0)
         tab2_sc_win = held([P, T3], U8, "tab2_sc_win")
-        zero(tab2_sc_win)
+        nc.gpsimd.memset(tab2_sc_win[:].bitcast(I32), 0)
         v_sc = [held([P, S], U8, "v_sc%d" % a) for a in range(PASSES)]
         w4_sc = [held([P, H], U8, "w4_sc%d" % a) for a in range(PASSES)]
         for a in range(1, PASSES):
             zero(v_sc[a])
             zero(w4_sc[a])
 
-        def load_w1(a):
-            raw = stream.tile([P, PACK, H], F32, name="w1_raw%d" % a, tag="stream")
-            nc.sync.dma_start(out=raw[:], in_=w1[a * 512 : (a + 1) * 512, :].rearrange("(p j) c -> p j c", j=PACK))
+        def load_w1(a, first, count):
+            raw = stream.tile([P, PACK, count], F32, name="w1_raw%d" % a, tag="stream")
+            rows = w1[a * 512 : (a + 1) * 512, first : first + count]
+            nc.sync.dma_start(out=raw[:], in_=rows.rearrange("(p j) c -> p j c", j=PACK))
             return raw
 
-        v = [[held([P, BANK], U32, "bands%d_%d" % (a, hf)) for hf in range(HALVES)] for a in range(PASSES)]
-        v2 = [held([P, BANK], U32, "samples%d" % hf) for hf in range(HALVES)]
+        v = [held([P, S], U32, "bands%d" % a) for a in range(PASSES)]
+        v2 = {}
         w1_codes = [held([P, H], U32, "w1_codes%d" % a) for a in range(PASSES)]
         w1_sc = [held([P, H], U8, "w1_sc%d" % a) for a in range(PASSES)]
         w1_bf = [held([P, PACK * H], BF16, "w1_bf%d" % a) for a in range(PASSES)]
         w4_codes = [held([P, H], U16, "w4_codes%d" % a) for a in range(PASSES)]
 
-        def round_w1(a, raw):
+        def round_w1(a, raw, first):
+            m0, m1 = first // PACK, (first + raw.shape[2]) // PACK
             nc.scalar.copy(
-                out=w1_bf[a][:].rearrange("p (t m j) -> p m j t", t=PACK, j=PACK),
+                out=w1_bf[a][:].rearrange("p (t m j) -> p m j t", t=PACK, j=PACK)[:, m0:m1],
                 in_=raw[:].rearrange("p j (m t) -> p m j t", t=PACK),
             )
 
@@ -115,14 +118,13 @@ def tile_list_infrared_window_scores_kernel(
             )
 
         def reading(bank, c, a, codes, scales, dtype, moving_scales):
-            hf, n0 = divmod(c * CHUNK, BANK)
             for t in range(PACK):
                 cols = slice(t * P, (t + 1) * P)
                 nc.tensor.matmul_mx(
                     out=bank[:, t * CHUNK : (t + 1) * CHUNK],
                     lhsT=codes[:, cols].bitcast(dtype),
                     lhsT_scale=scales[:, cols],
-                    rhs=v[a][hf][:, n0 : n0 + CHUNK].bitcast(FP8X4),
+                    rhs=v[a][:, c * CHUNK : (c + 1) * CHUNK].bitcast(FP8X4),
                     rhs_scale=moving_scales[:, c * CHUNK : (c + 1) * CHUNK],
                     start=(a == 0 and t == 0),
                     stop=(a == PASSES - 1 and t == PACK - 1),
@@ -150,7 +152,10 @@ def tile_list_infrared_window_scores_kernel(
 
         def join(c):
             hf, n0 = divmod(c * CHUNK, BANK)
-            f2 = ring.tile([P, BANK], F32, name="f2")
+            if c in (1, 3):
+                f2 = keep.tile([P, BANK], F32, name="f2_then_samples", tag="samples%d" % (c // 2), align_bytes=64)
+            else:
+                f2 = ring.tile([P, BANK], F32, name="f2")
             nc.scalar.copy(out=f2[:].rearrange("p (n t) -> p n t", t=PACK), in_=woven(f2_banks[c]))
             nc.vector.tensor_tensor(
                 out=h_bf[hf][:, PACK * n0 : PACK * (n0 + CHUNK)].rearrange("p (n t) -> p n t", t=PACK),
@@ -165,18 +170,21 @@ def tile_list_infrared_window_scores_kernel(
         first_chunks = range(CHUNKS // HALVES)
 
         idx = load_list(offs, "idx")
-        load_scale_rows(nc.gpsimd, tab_sc_win, tab_scales)
-        win = load_words(tab_words[0], "tab_win0")
-        raw = load_w1(0)
-        load_scale_rows(nc.gpsimd, w4_sc_raw, w4_scales)
-        idx2 = load_list(offs2, "idx2")
-        load_scale_rows(nc.sync, tab2_sc_win, tab2_scales)
+        wins = [load_words(tab_words[0], "tab_win0")]
+        load_scale_rows(tab_sc_win, tab_scales)
+        raws = [load_w1(0, 0, H)]
         w4_raw = held([P, PASSES, H // 2], I32, "w4_raw")
         nc.sync.dma_start(out=w4_raw[:], in_=w4_words.rearrange("a p c -> p a c").bitcast(I32))
-        for hf in range(HALVES):
-            gather_words(v[0][hf], win, idx, hf * BANK, BANK)
+        load_scale_rows(w4_sc_raw, w4_scales)
+        idx2 = load_list(offs2, "idx2")
+        wins.append(load_words(tab_words[1], "tab_win1"))
+        load_scale_rows(tab2_sc_win, tab2_scales)
+        raws.append(load_w1(1, 0, H))
+        raws.append(load_w1(2, 0, H))
+
+        gather_words(v[0][:], wins[0], idx, 0, S)
         nc.vector.tensor_copy(out=v_sc[0][:], in_=tab_sc_win[:].indirect(idx[:]))
-        round_w1(0, raw)
+        round_w1(0, raws[0], 0)
         quantize_w1(0)
         nc.vector.tensor_copy(
             out=w4_sc[0][:].rearrange("p (t m) -> p t m", t=PACK),
@@ -185,27 +193,9 @@ def tile_list_infrared_window_scores_kernel(
         for a in range(PASSES):
             deal_w4(a)
         for a in range(1, PASSES):
-            shift_rows(v_sc[a], v_sc[0], a)
-            shift_rows(w4_sc[a], w4_sc[0], a)
-        for c in first_chunks:
-            f2_pass(c, 0)
-            f1_pass(c, 0)
-
-        win = load_words(tab_words[1], "tab_win1")
-        raw = load_w1(1)
-        for hf in range(HALVES):
-            gather_words(v[1][hf], win, idx, hf * BANK, BANK)
-        round_w1(1, raw)
-        quantize_w1(1)
-        v2_sc = held([P, S2], U8, "v2_sc")
-        nc.vector.tensor_copy(out=v2_sc[:], in_=tab2_sc_win[:].indirect(idx2[:]))
-        for c in first_chunks:
-            f2_pass(c, 1)
-        for c in first_chunks:
-            f1_pass(c, 1)
-
-        raw = load_w1(2)
-        win = load_words(tab_words[2], "tab_win2")
+            shift_rows(v_sc[a], v_sc[0], 4 * a)
+            shift_rows(w4_sc[a], w4_sc[0], 4 * a)
+        wins.append(load_words(tab_words[2], "tab_win2"))
         tab2_win = load_words(tab2_words[0], "tab2_win")
         p1 = load_list(pos1, "p1")
         p2 = load_list(pos2, "p2")
@@ -214,19 +204,39 @@ def tile_list_infrared_window_scores_kernel(
         with nc.allow_non_contiguous_dma(reason="one value a row, a row a partition"):
             for cols, vec in ((steep_c, steep), (share_c, share), (base_c, base)):
                 nc.sync.dma_start(out=cols, in_=vec.rearrange("(m p) -> p m", p=P))
-        round_w1(2, raw)
+
+        for c in first_chunks:
+            f2_pass(c, 0)
+            f1_pass(c, 0)
+
+        gather_words(v[1][:], wins[1], idx, 0, S)
+        round_w1(1, raws[1], 0)
+        quantize_w1(1)
+        v2_sc = held([P, S2], U8, "v2_sc")
+        nc.vector.tensor_copy(out=v2_sc[:], in_=tab2_sc_win[:].indirect(idx2[:]))
+        for c in first_chunks:
+            f1_pass(c, 1)
+        for c in first_chunks:
+            f2_pass(c, 1)
+
+        round_w1(2, raws[2], 0)
         quantize_w1(2)
-        gather_words(v[2][0], win, idx, 0, BANK // 2)
-        gather_words(v[2][0], win, idx, BANK // 2, BANK // 2)
+        for first in (0, BANK // 2):
+            gather_words(v[2][:, first : first + BANK // 2], wins[2], idx, first, BANK // 2)
+
+        def gather_samples(part):
+            v2[part] = keep.tile([P, BANK], U32, name="samples", tag="samples%d" % part, align_bytes=64)
+            gather_words(v2[part][:], tab2_win, idx2, part * BANK, BANK)
+
         for c in first_chunks:
             f2_pass(c, 2)
             f1_pass(c, 2)
-            join(c)
             if c == 0:
-                gather_words(v[2][1], win, idx, BANK, BANK)
-        gather_words(v2[0], tab2_win, idx2, 0, BANK)
+                gather_words(v[2][:, BANK:S], wins[2], idx, BANK, BANK)
+            join(c)
+        gather_samples(0)
         quantize_h(0)
-        gather_words(v2[1], tab2_win, idx2, BANK, BANK)
+        gather_samples(1)
         slope = held([P, ROW_TILES], F32, "slope")
         steep_share = held([P, ROW_TILES], F32, "steep_share")
         nc.gpsimd.tensor_tensor(out=steep_share[:], in0=steep_c, in1=share_c, op=ALU.mult)
@@ -234,6 +244,10 @@ def tile_list_infrared_window_scores_kernel(
             out=slope[:], in0=steep_share[:], scalar1=-1.0, scalar2=0.0, op0=ALU.mult, op1=ALU.add
         )
 
+        neg_base = held([P, ROW_TILES], F32, "neg_base")
+        nc.gpsimd.tensor_scalar(
+            out=neg_base[:], in0=base_c, scalar1=-1.0, scalar2=0.0, op0=ALU.mult, op1=ALU.add
+        )
         half_top = held([P, ROW_TILES, HALVES], F32, "half_top")
         gate_bias = held([P, ROW_TILES], F32, "gate_bias")
         scores = {}
@@ -264,22 +278,29 @@ def tile_list_infrared_window_scores_kernel(
                 out=gate_bias[:, m : m + 1], in0=half_top[:, m, 0:1], scalar1=half_top[:, m, 1:2],
                 scalar2=slope[:, m : m + 1], op0=ALU.max, op1=ALU.mult,
             )
-            gates[m] = ring.tile([P, PICK], F32, name="gate")
+            gates[m] = ring.tile([P, PICK], F32, name="gate", bufs=ROW_TILES)
             nc.scalar.activation(
                 out=gates[m][:], in_=scores[m][:].indirect(p1[:]), func=ACT.Sigmoid,
                 bias=gate_bias[:, m : m + 1], scale=steep_c[:, m : m + 1],
             )
 
         def pick(m):
-            picked[m] = ring.tile([P, PICK], F32, name="picked")
+            picked[m] = ring.tile([P, PICK], F32, name="picked", bufs=6)
             nc.vector.tensor_copy(out=picked[m][:], in_=scores[m][:].indirect(p2[:]))
 
         def finish(m):
-            result = ring.tile([P, PICK], F32, name="result")
-            nc.vector.scalar_tensor_tensor(
-                out=result[:], in0=picked[m][:], scalar=base_c[:, m : m + 1], in1=gates[m][:],
-                op0=ALU.subtract, op1=ALU.mult,
-            )
+            result = ring.tile([P, PICK], F32, name="result", bufs=4)
+            if m >= ROW_TILES - VECTOR_FINISHES:
+                nc.vector.scalar_tensor_tensor(
+                    out=result[:], in0=picked[m][:], scalar=base_c[:, m : m + 1], in1=gates[m][:],
+                    op0=ALU.subtract, op1=ALU.mult,
+                )
+            else:
+                above = ring.tile([P, PICK], F32, name="above", bufs=4)
+                nc.scalar.activation(
+                    out=above[:], in_=picked[m][:], func=ACT.Identity, bias=neg_base[:, m : m + 1], scale=1.0
+                )
+                nc.gpsimd.tensor_tensor(out=result[:], in0=above[:], in1=gates[m][:], op=ALU.mult)
             nc.sync.dma_start(out=out[m * P : (m + 1) * P, :], in_=result[:])
 
         def chunk(c):
@@ -294,12 +315,10 @@ def tile_list_infrared_window_scores_kernel(
         for m in range(0, 4):
             score(m, 0)
         chunk(6)
-        for m in range(4, 6):
-            score(m, 0)
         chunk(7)
-        score(6, 0)
+        score(4, 0)
         quantize_h(1)
-        score(7, 0)
+        score(5, 0)
         score(0, 1)
         look(0)
         for m in range(ROW_TILES):
@@ -307,6 +326,8 @@ def tile_list_infrared_window_scores_kernel(
                 score(m + 1, 1)
                 look(m + 1)
             pick(m)
+            if m + 6 < ROW_TILES:
+                score(m + 6, 0)
             if m > 0:
                 finish(m - 1)
         finish(ROW_TILES - 1)

@@ -26,7 +26,8 @@ CHUNKS = S // CHUNK
 ROW_TILES = S2 // P
 LIVE_ROWS = 100
 STREAM_BUFS = 5
-VECTOR_FINISHES = 1
+VECTOR_FINISHES = 2
+PAIR = 2
 
 
 def tile_list_infrared_window_scores_kernel(
@@ -144,7 +145,7 @@ def tile_list_infrared_window_scores_kernel(
             reading(f2_banks[c], c, a, w4_codes[a], w4_sc[a], FP4X4, v_sc[a])
 
         def woven(bank):
-            return bank[:].rearrange("p (t n) -> p n t", t=PACK)
+            return bank[:].rearrange("p (t n e) -> p n t e", t=PACK, e=PAIR)
 
         h_bf = [held([P, PACK * BANK], BF16, "h_bf%d" % hf) for hf in range(HALVES)]
         h_codes = [held([P, BANK], U32, "h_codes%d" % hf) for hf in range(HALVES)]
@@ -156,11 +157,11 @@ def tile_list_infrared_window_scores_kernel(
                 f2 = keep.tile([P, BANK], F32, name="f2_then_samples", tag="samples%d" % (c // 2), align_bytes=64)
             else:
                 f2 = ring.tile([P, BANK], F32, name="f2")
-            nc.scalar.copy(out=f2[:].rearrange("p (n t) -> p n t", t=PACK), in_=woven(f2_banks[c]))
+            nc.scalar.copy(out=f2[:].rearrange("p (n t e) -> p n t e", t=PACK, e=PAIR), in_=woven(f2_banks[c]))
             nc.vector.tensor_tensor(
-                out=h_bf[hf][:, PACK * n0 : PACK * (n0 + CHUNK)].rearrange("p (n t) -> p n t", t=PACK),
+                out=h_bf[hf][:, PACK * n0 : PACK * (n0 + CHUNK)].rearrange("p (n e t) -> p n t e", t=PACK, e=PAIR),
                 in0=woven(f1_banks[c]),
-                in1=f2[:].rearrange("p (n t) -> p n t", t=PACK),
+                in1=f2[:].rearrange("p (n t e) -> p n t e", t=PACK, e=PAIR),
                 op=ALU.max,
             )
 
@@ -221,8 +222,7 @@ def tile_list_infrared_window_scores_kernel(
 
         round_w1(2, raws[2], 0)
         quantize_w1(2)
-        for first in (0, BANK // 2):
-            gather_words(v[2][:, first : first + BANK // 2], wins[2], idx, first, BANK // 2)
+        gather_words(v[2][:, 0:BANK], wins[2], idx, 0, BANK)
 
         def gather_samples(part):
             v2[part] = keep.tile([P, BANK], U32, name="samples", tag="samples%d" % part, align_bytes=64)

@@ -170,17 +170,17 @@ def tile_list_infrared_window_scores_kernel(
 
         first_chunks = range(CHUNKS // HALVES)
 
-        idx = load_list(offs, "idx")
         wins = [load_words(tab_words[0], "tab_win0")]
-        load_scale_rows(tab_sc_win, tab_scales)
+        idx = load_list(offs, "idx")
         raws = [load_w1(0, 0, H)]
+        load_scale_rows(tab_sc_win, tab_scales)
         w4_raw = held([P, PASSES, H // 2], I32, "w4_raw")
         nc.sync.dma_start(out=w4_raw[:], in_=w4_words.rearrange("a p c -> p a c").bitcast(I32))
+        wins.append(load_words(tab_words[1], "tab_win1"))
         load_scale_rows(w4_sc_raw, w4_scales)
         idx2 = load_list(offs2, "idx2")
-        wins.append(load_words(tab_words[1], "tab_win1"))
-        load_scale_rows(tab2_sc_win, tab2_scales)
         raws.append(load_w1(1, 0, H))
+        load_scale_rows(tab2_sc_win, tab2_scales)
         raws.append(load_w1(2, 0, H))
 
         gather_words(v[0][:], wins[0], idx, 0, S)
@@ -193,10 +193,11 @@ def tile_list_infrared_window_scores_kernel(
         )
         for a in range(PASSES):
             deal_w4(a)
-        for a in range(1, PASSES):
-            shift_rows(v_sc[a], v_sc[0], 4 * a)
-            shift_rows(w4_sc[a], w4_sc[0], 4 * a)
+        shift_rows(v_sc[1], v_sc[0], 4)
+        shift_rows(w4_sc[1], w4_sc[0], 4)
         wins.append(load_words(tab_words[2], "tab_win2"))
+        shift_rows(v_sc[2], v_sc[0], 8)
+        shift_rows(w4_sc[2], w4_sc[0], 8)
         tab2_win = load_words(tab2_words[0], "tab2_win")
         p1 = load_list(pos1, "p1")
         p2 = load_list(pos2, "p2")
@@ -269,15 +270,18 @@ def tile_list_infrared_window_scores_kernel(
                 stop=True,
             )
             nc.vector.tensor_scalar(
-                out=scores[m][:, hf * BANK : (hf + 1) * BANK], in0=bank[:], scalar1=1.0, scalar2=None,
+                out=scores[m][:, hf * BANK : (hf + 1) * BANK], in0=bank[:], scalar1=1.0,
+                scalar2=None if hf == 0 else half_top[:, m, 0:1],
                 op0=ALU.mult, op1=ALU.max, accum_out=half_top[:, m, hf : hf + 1],
             )
 
-        def look(m):
+        def bias(m):
             nc.gpsimd.tensor_scalar(
-                out=gate_bias[:, m : m + 1], in0=half_top[:, m, 0:1], scalar1=half_top[:, m, 1:2],
-                scalar2=slope[:, m : m + 1], op0=ALU.max, op1=ALU.mult,
+                out=gate_bias[:, m : m + 1], in0=half_top[:, m, 1:2], scalar1=slope[:, m : m + 1],
+                scalar2=0.0, op0=ALU.mult, op1=ALU.add,
             )
+
+        def look(m):
             gates[m] = ring.tile([P, PICK], F32, name="gate", bufs=ROW_TILES)
             nc.scalar.activation(
                 out=gates[m][:], in_=scores[m][:].indirect(p1[:]), func=ACT.Sigmoid,
@@ -320,14 +324,17 @@ def tile_list_infrared_window_scores_kernel(
         quantize_h(1)
         score(5, 0)
         score(0, 1)
+        bias(0)
         look(0)
         for m in range(ROW_TILES):
             if m + 1 < ROW_TILES:
                 score(m + 1, 1)
-                look(m + 1)
+                bias(m + 1)
             pick(m)
             if m + 6 < ROW_TILES:
                 score(m + 6, 0)
             if m > 0:
                 finish(m - 1)
+            if m + 1 < ROW_TILES:
+                look(m + 1)
         finish(ROW_TILES - 1)

from contextlib import ExitStack

import concourse.mybir as mybir

K, T, S, H, T3, S2, PICK = 1536, 2048, 1024, 512, 2048, 1024, 512
FLOPS = 2 * (2 * K * H * S) + 2 * H * S2 * S

F32 = mybir.dt.float32
BF16 = mybir.dt.bfloat16
I32 = mybir.dt.int32
U32 = mybir.dt.uint32
U16 = mybir.dt.uint16
U8 = mybir.dt.uint8
FP8X4 = mybir.dt.float8_e4m3fn_x4
FP4X4 = mybir.dt.float4_e2m1fn_x4
ALU = mybir.AluOpType
ACT = mybir.ActivationFunctionType

P = 128
PACK = 4
PASSES = K // (P * PACK)
BANK = 512
HALVES = S // BANK
CHUNK = BANK // PACK
CHUNKS = S // CHUNK
ROW_TILES = S2 // P
LIVE_ROWS = 100
STREAM_BUFS = 5
VECTOR_FINISHES = 2
PAIR = 2


def tile_list_infrared_window_scores_kernel(
    tc, tab_words, tab_scales, offs, tab2_words, tab2_scales, offs2, pos1, pos2,
    w1, w4_words, w4_scales, steep, share, base, out,
):
    nc = tc.nc
    with ExitStack() as ctx:
        lists = ctx.enter_context(tc.tile_pool(name="lists", bufs=1))
        keep = ctx.enter_context(tc.tile_pool(name="keep", bufs=1))
        stream = ctx.enter_context(tc.tile_pool(name="stream", bufs=STREAM_BUFS))
        ring = ctx.enter_context(tc.tile_pool(name="ring", bufs=3))
        psum = ctx.enter_context(tc.psum_pool(name="psum", bufs=8))

        def held(shape, dtype, name):
            return keep.tile(shape, dtype, name=name, align_bytes=64)

        def zero(tile):
            nc.vector.memset(tile[:].bitcast(I32), 0)

        def load_list(src, name):
            tile = lists.tile(list(src.shape), U16, name=name)
            nc.sync.dma_start(tile[:], src)
            return tile

        def load_scale_rows(tile, scales):
            passes = scales.shape[0]
            for q in range(4):
                nc.sync.dma_start(
                    out=tile[32 * q : 32 * q + 4 * passes, :].bitcast(I32),
                    in_=scales[:, 4 * q : 4 * q + 4, :].bitcast(I32),
                )

        def load_words(words, name):
            tile = stream.tile([P, T], I32, name=name, tag="stream")
            nc.sync.dma_start(out=tile[:], in_=words.rearrange("p t i -> p (t i)").bitcast(I32))
            return tile

        def gather_words(dst, window, index, first, count):
            nc.vector.tensor_copy(
                out=dst,
                in_=window[:].bitcast(U32).indirect(index[:, first // 16 : (first + count) // 16]),
            )

        def shift_rows(dst, src, first):
            nc.sync.dma_start(
                out=dst[0:LIVE_ROWS, :].bitcast(I32), in_=src[first : first + LIVE_ROWS, :].bitcast(I32)
            )

        tab_sc_win = held([P, T], U8, "tab_sc_win")
        nc.gpsimd.memset(tab_sc_win[:].bitcast(I32), 0)
        w4_sc_raw = held([P, H], U8, "w4_sc_raw")
        nc.gpsimd.memset(w4_sc_raw[:].bitcast(I32), 0)
        tab2_sc_win = held([P, T3], U8, "tab2_sc_win")
        nc.gpsimd.memset(tab2_sc_win[:].bitcast(I32), 0)
        v_sc = [held([P, S], U8, "v_sc%d" % a) for a in range(PASSES)]
        w4_sc = [held([P, H], U8, "w4_sc%d" % a) for a in range(PASSES)]
        for a in range(1, PASSES):
            zero(v_sc[a])
            zero(w4_sc[a])

        def load_w1(a, first, count):
            raw = stream.tile([P, PACK, count], F32, name="w1_raw%d" % a, tag="stream")
            rows = w1[a * 512 : (a + 1) * 512, first : first + count]
            nc.sync.dma_start(out=raw[:], in_=rows.rearrange("(p j) c -> p j c", j=PACK))
            return raw

        v = [held([P, S], U32, "bands%d" % a) for a in range(PASSES)]
        v2 = {}
        w1_codes = [held([P, H], U32, "w1_codes%d" % a) for a in range(PASSES)]
        w1_sc = [held([P, H], U8, "w1_sc%d" % a) for a in range(PASSES)]
        w1_bf = [held([P, PACK * H], BF16, "w1_bf%d" % a) for a in range(PASSES)]
        w4_codes = [held([P, H], U16, "w4_codes%d" % a) for a in range(PASSES)]

        def round_w1(a, raw, first):
            m0, m1 = first // PACK, (first + raw.shape[2]) // PACK
            nc.scalar.copy(
                out=w1_bf[a][:].rearrange("p (t m j) -> p m j t", t=PACK, j=PACK)[:, m0:m1],
                in_=raw[:].rearrange("p j (m t) -> p m j t", t=PACK),
            )

        def quantize_w1(a):
            nc.vector.quantize_mx(out=w1_codes[a][:].bitcast(FP8X4), scales=w1_sc[a][:], in_=w1_bf[a][:])

        def deal_w4(a):
            nc.scalar.copy(
                out=w4_codes[a][:].rearrange("p (t m) -> p t m", t=PACK),
                in_=w4_raw[:, a, :].bitcast(U16).rearrange("p (m t) -> p t m", t=PACK),
            )

        def reading(bank, c, a, codes, scales, dtype, moving_scales):
            for t in range(PACK):
                cols = slice(t * P, (t + 1) * P)
                nc.tensor.matmul_mx(
                    out=bank[:, t * CHUNK : (t + 1) * CHUNK],
                    lhsT=codes[:, cols].bitcast(dtype),
                    lhsT_scale=scales[:, cols],
                    rhs=v[a][:, c * CHUNK : (c + 1) * CHUNK].bitcast(FP8X4),
                    rhs_scale=moving_scales[:, c * CHUNK : (c + 1) * CHUNK],
                    start=(a == 0 and t == 0),
                    stop=(a == PASSES - 1 and t == PACK - 1),
                )

        f1_banks = {}
        f2_banks = {}

        def f1_pass(c, a):
            if a == 0:
                f1_banks[c] = psum.tile([P, BANK], F32, name="bank")
            reading(f1_banks[c], c, a, w1_codes[a], w1_sc[a], FP8X4, v_sc[0][4 * a : P, :])

        def f2_pass(c, a):
            if a == 0:
                f2_banks[c] = psum.tile([P, BANK], F32, name="bank")
            reading(f2_banks[c], c, a, w4_codes[a], w4_sc[a], FP4X4, v_sc[a])

        def woven(bank):
            return bank[:].rearrange("p (t n e) -> p n t e", t=PACK, e=PAIR)

        h_bf = [held([P, PACK * BANK], BF16, "h_bf%d" % hf) for hf in range(HALVES)]
        h_codes = [held([P, BANK], U32, "h_codes%d" % hf) for hf in range(HALVES)]
        h_sc = [held([P, BANK], U8, "h_sc%d" % hf) for hf in range(HALVES)]

        def join(c):
            hf, n0 = divmod(c * CHUNK, BANK)
            if c in (1, 3):
                f2 = keep.tile([P, BANK], F32, name="f2_then_samples", tag="samples%d" % (c // 2), align_bytes=64)
            else:
                f2 = ring.tile([P, BANK], F32, name="f2")
            nc.scalar.copy(out=f2[:].rearrange("p (n t e) -> p n t e", t=PACK, e=PAIR), in_=woven(f2_banks[c]))
            nc.vector.tensor_tensor(
                out=h_bf[hf][:, PACK * n0 : PACK * (n0 + CHUNK)].rearrange("p (n e t) -> p n t e", t=PACK, e=PAIR),
                in0=woven(f1_banks[c]),
                in1=f2[:].rearrange("p (n t e) -> p n t e", t=PACK, e=PAIR),
                op=ALU.max,
            )

        def quantize_h(hf):
            nc.vector.quantize_mx(out=h_codes[hf][:].bitcast(FP8X4), scales=h_sc[hf][:], in_=h_bf[hf][:])

        first_chunks = range(CHUNKS // HALVES)

        wins = [load_words(tab_words[0], "tab_win0")]
        idx = load_list(offs, "idx")
        raws = [load_w1(0, 0, H)]
        load_scale_rows(tab_sc_win, tab_scales)
        w4_raw = held([P, PASSES, H // 2], I32, "w4_raw")
        nc.sync.dma_start(out=w4_raw[:], in_=w4_words.rearrange("a p c -> p a c").bitcast(I32))
        wins.append(load_words(tab_words[1], "tab_win1"))
        load_scale_rows(w4_sc_raw, w4_scales)
        idx2 = load_list(offs2, "idx2")
        raws.append(load_w1(1, 0, H))
        load_scale_rows(tab2_sc_win, tab2_scales)
        raws.append(load_w1(2, 0, H))

        gather_words(v[0][:], wins[0], idx, 0, S)
        nc.vector.tensor_copy(out=v_sc[0][:], in_=tab_sc_win[:].indirect(idx[:]))
        round_w1(0, raws[0], 0)
        quantize_w1(0)
        nc.vector.tensor_copy(
            out=w4_sc[0][:].rearrange("p (t m) -> p t m", t=PACK),
            in_=w4_sc_raw[:].rearrange("p (m t) -> p t m", t=PACK),
        )
        for a in range(PASSES):
            deal_w4(a)
        shift_rows(v_sc[1], v_sc[0], 4)
        shift_rows(w4_sc[1], w4_sc[0], 4)
        wins.append(load_words(tab_words[2], "tab_win2"))
        shift_rows(v_sc[2], v_sc[0], 8)
        shift_rows(w4_sc[2], w4_sc[0], 8)
        tab2_win = load_words(tab2_words[0], "tab2_win")
        p1 = load_list(pos1, "p1")
        p2 = load_list(pos2, "p2")
        rowwise = stream.tile([P, 3, ROW_TILES], F32, name="rowwise", tag="stream")
        steep_c, share_c, base_c = rowwise[:, 0, :], rowwise[:, 1, :], rowwise[:, 2, :]
        with nc.allow_non_contiguous_dma(reason="one value a row, a row a partition"):
            for cols, vec in ((steep_c, steep), (share_c, share), (base_c, base)):
                nc.sync.dma_start(out=cols, in_=vec.rearrange("(m p) -> p m", p=P))

        for c in first_chunks:
            f2_pass(c, 0)
            f1_pass(c, 0)

        gather_words(v[1][:], wins[1], idx, 0, S)
        round_w1(1, raws[1], 0)
        quantize_w1(1)
        v2_sc = held([P, S2], U8, "v2_sc")
        nc.vector.tensor_copy(out=v2_sc[:], in_=tab2_sc_win[:].indirect(idx2[:]))
        for c in first_chunks:
            f1_pass(c, 1)
        for c in first_chunks:
            f2_pass(c, 1)

        round_w1(2, raws[2], 0)
        quantize_w1(2)
        gather_words(v[2][:, 0:BANK], wins[2], idx, 0, BANK)

        def gather_samples(part):
            v2[part] = keep.tile([P, BANK], U32, name="samples", tag="samples%d" % part, align_bytes=64)
            gather_words(v2[part][:], tab2_win, idx2, part * BANK, BANK)

        for c in first_chunks:
            f2_pass(c, 2)
            f1_pass(c, 2)
            if c == 0:
                gather_words(v[2][:, BANK:S], wins[2], idx, BANK, BANK)
            join(c)
        gather_samples(0)
        quantize_h(0)
        gather_samples(1)
        slope = held([P, ROW_TILES], F32, "slope")
        steep_share = held([P, ROW_TILES], F32, "steep_share")
        nc.gpsimd.tensor_tensor(out=steep_share[:], in0=steep_c, in1=share_c, op=ALU.mult)
        nc.gpsimd.tensor_scalar(
            out=slope[:], in0=steep_share[:], scalar1=-1.0, scalar2=0.0, op0=ALU.mult, op1=ALU.add
        )

        neg_base = held([P, ROW_TILES], F32, "neg_base")
        nc.gpsimd.tensor_scalar(
            out=neg_base[:], in0=base_c, scalar1=-1.0, scalar2=0.0, op0=ALU.mult, op1=ALU.add
        )
        half_top = held([P, ROW_TILES, HALVES], F32, "half_top")
        gate_bias = held([P, ROW_TILES], F32, "gate_bias")
        scores = {}
        gates = {}
        picked = {}

        def score(m, hf):
            if hf == 0:
                scores[m] = ring.tile([P, S], F32, name="scores", bufs=ROW_TILES)
            part, m0 = divmod(m * P, BANK)
            bank = psum.tile([P, BANK], F32, name="bank")
            nc.tensor.matmul_mx(
                out=bank[:],
                lhsT=v2[part][:, m0 : m0 + P].bitcast(FP8X4),
                lhsT_scale=v2_sc[:, m * P : (m + 1) * P],
                rhs=h_codes[hf][:].bitcast(FP8X4),
                rhs_scale=h_sc[hf][:],
                start=True,
                stop=True,
            )
            nc.vector.tensor_scalar(
                out=scores[m][:, hf * BANK : (hf + 1) * BANK], in0=bank[:], scalar1=1.0,
                scalar2=None if hf == 0 else half_top[:, m, 0:1],
                op0=ALU.mult, op1=ALU.max, accum_out=half_top[:, m, hf : hf + 1],
            )

        def bias(m):
            nc.gpsimd.tensor_scalar(
                out=gate_bias[:, m : m + 1], in0=half_top[:, m, 1:2], scalar1=slope[:, m : m + 1],
                scalar2=0.0, op0=ALU.mult, op1=ALU.add,
            )

        def look(m):
            gates[m] = ring.tile([P, PICK], F32, name="gate", bufs=ROW_TILES)
            nc.scalar.activation(
                out=gates[m][:], in_=scores[m][:].indirect(p1[:]), func=ACT.Sigmoid,
                bias=gate_bias[:, m : m + 1], scale=steep_c[:, m : m + 1],
            )

        def pick(m):
            picked[m] = ring.tile([P, PICK], F32, name="picked", bufs=6)
            nc.vector.tensor_copy(out=picked[m][:], in_=scores[m][:].indirect(p2[:]))

        def finish(m):
            result = ring.tile([P, PICK], F32, name="result", bufs=4)
            if m >= ROW_TILES - VECTOR_FINISHES:
                nc.vector.scalar_tensor_tensor(
                    out=result[:], in0=picked[m][:], scalar=base_c[:, m : m + 1], in1=gates[m][:],
                    op0=ALU.subtract, op1=ALU.mult,
                )
            else:
                above = ring.tile([P, PICK], F32, name="above", bufs=4)
                nc.scalar.activation(
                    out=above[:], in_=picked[m][:], func=ACT.Identity, bias=neg_base[:, m : m + 1], scale=1.0
                )
                nc.gpsimd.tensor_tensor(out=result[:], in0=above[:], in1=gates[m][:], op=ALU.mult)
            nc.sync.dma_start(out=out[m * P : (m + 1) * P, :], in_=result[:])

        def chunk(c):
            for a in range(PASSES):
                f2_pass(c, a)
            for a in range(PASSES):
                f1_pass(c, a)
            join(c)

        chunk(4)
        chunk(5)
        for m in range(0, 4):
            score(m, 0)
        chunk(6)
        chunk(7)
        score(4, 0)
        quantize_h(1)
        score(5, 0)
        score(0, 1)
        bias(0)
        look(0)
        for m in range(ROW_TILES):
            if m + 1 < ROW_TILES:
                score(m + 1, 1)
                bias(m + 1)
            pick(m)
            if m + 6 < ROW_TILES:
                score(m + 6, 0)
            if m > 0:
                finish(m - 1)
            if m + 1 < ROW_TILES:
                look(m + 1)
        finish(ROW_TILES - 1)
